import numpy as np
import ml_dtypes


def mxq(x, axis, fmt="e4m3"):
    dtype, down = {"e4m3": (ml_dtypes.float8_e4m3fn, 7), "e5m2": (ml_dtypes.float8_e5m2, 14)}[fmt]
    v = np.moveaxis(np.asarray(x, np.float32).astype(ml_dtypes.bfloat16).astype(np.float64), axis, -1)
    blocks = v.reshape(v.shape[:-1] + (-1, 32))
    amax = np.abs(blocks).max(-1, keepdims=True)
    byte = np.maximum(np.where(amax > 0, np.frexp(amax)[1] - 1 + 127, 0) - down, 1)
    scale = np.exp2(byte - 127.0)
    codes = (blocks / scale).astype(np.float32).astype(dtype).astype(np.float64)
    return np.moveaxis((codes * scale).reshape(v.shape), -1, axis)


WIDE = False


def mx_kscale(k):
    if not WIDE:
        return np.ones(k)
    levels = np.array([30, -30])
    if k % 512:
        return np.exp2(np.random.permutation(np.resize(levels, k // 32))).repeat(32)
    a = np.empty((k // 512, 16))
    for p in range(k // 512):
        a[p, :8] = np.random.permutation(np.resize(levels, 8))
        for g in range(8):
            far = levels[np.abs(levels - a[p, g]) >= 10]
            a[p, g + 8] = far[np.random.randint(len(far))]
    return np.exp2(a.ravel()).repeat(32)


def f64(x):
    return np.asarray(x).astype(np.float64)


def striped(idx):
    return np.tile(np.asarray(idx).reshape(-1, 16).T, (8, 1)).astype(np.uint16)


def unstriped(offs):
    return offs[:16].T.reshape(-1).astype(np.int64)


def striped8(idx):
    return np.asarray(idx).reshape(8, -1, 16).transpose(0, 2, 1).reshape(128, -1).astype(np.uint16)


def unstriped8(offs):
    return offs.reshape(8, 16, -1).transpose(0, 2, 1).reshape(8, -1).astype(np.int64)


def pick8(x, idx, run):
    r = np.arange(len(x))
    return x[r[:, None], idx[r % (8 * run) // run]]


K, J, N, T, V = 256, 1024, 256, 2048, 2048


def setup_inputs():
    n = np.random.standard_normal
    idx = np.stack([np.random.permutation(T)[:J] for _ in range(8)])
    idx2 = np.random.permutation(V)[:J]
    idx3 = np.random.permutation(V)[:J]
    fj = mx_kscale(J)
    return {
        "xf": (n((K, T))).astype(np.float32),
        "ra": (np.random.uniform(0.5, 1.5, (1, J)) * fj).astype(np.float32),
        "gt": (n((N, V)) * np.exp(0.5 * n((1, V)))).astype(np.float32),
        "rb": (np.random.uniform(0.5, 1.5, (1, J)) / fj).astype(np.float32),
        "mom": (1.0 * n((K, N))).astype(np.float32),
        "old": (1.0 * n((K, N))).astype(np.float32),
        "offs": striped8(idx),
        "offs2": striped(idx2),
        "offs3": striped(idx3),
    }


def reference(xf, ra, gt, rb, mom, old, offs, offs2, offs3):
    idx = unstriped8(offs)
    idx2 = unstriped(offs2)
    idx3 = unstriped(offs3)
    us = pick8(f64(xf), idx, 16) * f64(ra)
    uj = us.T
    gs = (f64(gt)[:, idx2] - 0.7 * f64(gt)[:, idx3]) * f64(rb)
    gj = gs.T
    ujq = mxq(uj, 0, "e4m3")
    gjq = mxq(gj, 0, "e5m2")
    w = ujq.T @ gjq
    u2 = 0.04 * w + 0.6 * f64(mom)
    y = f64(old) * 0.5 - u2 / (1.0 + np.abs(u2))
    return y

@@ -1,0 +1,202 @@
+from contextlib import ExitStack
+
+import concourse.mybir as mybir
+from concourse.masks import make_identity
+
+K, J, N, T = 256, 1024, 256, 2048
+FLOPS = 2 * K * J * N
+
+F32 = mybir.dt.float32
+BF16 = mybir.dt.bfloat16
+U32 = mybir.dt.uint32
+U16 = mybir.dt.uint16
+U8 = mybir.dt.uint8
+E4M3X4 = mybir.dt.float8_e4m3fn_x4
+E5M2X4 = mybir.dt.float8_e5m2_x4
+ALU = mybir.AluOpType
+ACT = mybir.ActivationFunctionType
+
+P = 128
+PACK = 4
+J_PASS = P * PACK
+PASSES = J // J_PASS
+LIST_ROWS = 16
+
+
+def tile_list_moment_headpicks_differences_momentum_kernel(tc, xf, ra, gt, rb, mom, old, offs, offs2, offs3, out):
+    nc = tc.nc
+    with ExitStack() as ctx:
+        lists = ctx.enter_context(tc.tile_pool(name="lists", bufs=1))
+        keep = ctx.enter_context(tc.tile_pool(name="keep", bufs=1))
+        turn = ctx.enter_context(tc.psum_pool(name="turn", bufs=4))
+        held = ctx.enter_context(tc.psum_pool(name="held", bufs=1))
+
+        list_x = lists.tile([P, J // LIST_ROWS], U16, name="list_x")
+        list_g2 = lists.tile([P, J // LIST_ROWS], U16, name="list_g2")
+        list_g3 = lists.tile([P, J // LIST_ROWS], U16, name="list_g3")
+        nc.sync.dma_start(list_g3[:], offs3)
+        nc.sync.dma_start(list_g2[:], offs2)
+
+        warm = keep.tile([P, 2], F32, name="warm")
+        nc.vector.memset(warm[:, 0:1], 1.0)
+        nc.scalar.activation(warm[:, 1:2], warm[:, 0:1], ACT.Abs_reciprocal_sqrt, bias=1.0, scale=0.04)
+
+        g_rows = [keep.tile([P, T], F32, name=f"g_rows{i}") for i in range(2)]
+        x_rows = [keep.tile([P, T], F32, name=f"x_rows{i}") for i in range(2)]
+        ra_col = keep.tile([P, PASSES, PACK], F32, name="ra_col")
+        rb_col = keep.tile([P, PASSES, PACK], F32, name="rb_col")
+        mom_sb = keep.tile([P, 2, N], F32, name="mom_sb")
+        old_sb = keep.tile([P, 2, N], F32, name="old_sb")
+        nc.sync.dma_start(g_rows[0][:], gt[0:P, :])
+        nc.sync.dma_start(rb_col[:], rb.rearrange("o (g p t) -> p (o g) t", p=P, t=PACK))
+        nc.sync.dma_start(ra_col[:], ra.rearrange("o (g p t) -> p (o g) t", p=P, t=PACK))
+        nc.sync.dma_start(list_x[:], offs)
+        nc.sync.dma_start(g_rows[1][:], gt[P : 2 * P, :])
+        nc.sync.dma_start(x_rows[0][:], xf[0:P, :])
+        nc.sync.dma_start(x_rows[1][:], xf[P : 2 * P, :])
+        nc.sync.dma_start(mom_sb[:], mom.rearrange("(i p) n -> p i n", p=P))
+        nc.sync.dma_start(old_sb[:], old.rearrange("(i p) n -> p i n", p=P))
+
+        ident = keep.tile([P, P], F32, name="ident")
+        make_identity(nc, ident[:])
+
+        def entries(lst, j0, j1):
+            return lst[:, j0 // LIST_ROWS : j1 // LIST_ROWS]
+
+        minus3 = [[keep.tile([P, J_PASS], F32, name=f"minus3_{i}{a}") for a in range(PASSES)] for i in range(2)]
+        diff = [[keep.tile([P, J_PASS], F32, name=f"diff_{i}{a}") for a in range(PASSES)] for i in range(2)]
+        picked = [[keep.tile([P, J_PASS], F32, name=f"picked_{i}{a}") for a in range(PASSES)] for i in range(2)]
+        g_bf = keep.tile([P, PASSES, N, PACK], BF16, name="g_bf", align_bytes=64)
+        g_codes = keep.tile([P, PASSES, N], U32, name="g_codes", align_bytes=64)
+        g_scales = keep.tile([P, PASSES, N], U8, name="g_scales", align_bytes=64)
+        u_bf = [keep.tile([P, PASSES, P, PACK], BF16, name=f"u_bf{i}", align_bytes=64) for i in range(2)]
+        u_codes = [keep.tile([P, PASSES, P], U32, name=f"u_codes{i}", align_bytes=64) for i in range(2)]
+        u_scales = [keep.tile([P, PASSES, P], U8, name=f"u_scales{i}", align_bytes=64) for i in range(2)]
+        acc = [held.tile([P, N], F32, name=f"acc{i}") for i in range(2)]
+        ra_row = [held.tile([P, PACK, P], F32, name=f"ra_row{a}") for a in range(PASSES)]
+
+        def gather_g3(i, a, c0, c1):
+            nc.scalar.activation(
+                minus3[i][a][:, c0:c1],
+                g_rows[i][:].indirect(entries(list_g3, a * J_PASS + c0, a * J_PASS + c1)),
+                ACT.Copy,
+                scale=-0.7,
+            )
+
+        def gather_g2(i, a, c0, c1):
+            nc.vector.tensor_tensor(
+                diff[i][a][:, c0:c1],
+                g_rows[i][:].indirect(entries(list_g2, a * J_PASS + c0, a * J_PASS + c1)),
+                minus3[i][a][:, c0:c1],
+                ALU.add,
+            )
+
+        def gather_x(i, a):
+            nc.scalar.activation(
+                picked[i][a][:],
+                x_rows[i][:].indirect(entries(list_x, a * J_PASS, (a + 1) * J_PASS)),
+                ACT.Copy,
+            )
+
+        def turn_and_weigh(src, weight_col, dst):
+            bank = turn.tile([P, PACK, P], F32, name="bank")
+            by_slot = src[:].rearrange("c (p t) -> c t p", t=PACK)
+            for t in range(PACK):
+                nc.tensor.transpose(bank[:, t, :], by_slot[:, t, :], ident[:])
+            nc.vector.tensor_tensor(
+                dst,
+                bank[:].rearrange("p t c -> p c t"),
+                weight_col.unsqueeze(1).to_broadcast([P, P, PACK]),
+                ALU.mult,
+            )
+
+        def weigh_and_turn(src, weight_row, dst, name):
+            rounded = keep.tile([P, P, PACK], BF16, name=name)
+            nc.vector.tensor_tensor(
+                rounded[:],
+                src[:].rearrange("c (p t) -> c p t", t=PACK),
+                weight_row[:].rearrange("c t p -> c p t"),
+                ALU.mult,
+            )
+            words = rounded[:].rearrange("c p t -> c (p t)").bitcast(F32).rearrange("c (p u) -> c u p", u=2)
+            bank = turn.tile([P, PACK, P], F32, name="bank")
+            for u in range(2):
+                nc.tensor.transpose(bank[:, u, :], words[:, u, :], ident[:])
+            nc.scalar.copy(
+                dst.rearrange("p c t -> p (c t)").bitcast(F32).rearrange("p (c u) -> p c u", u=2),
+                bank[:, 0:2, :].rearrange("p u c -> p c u"),
+            )
+
+        def quantize(codes, scales, values, fmt, a0, a1):
+            nc.vector.quantize_mx(
+                out=codes[:, a0:a1, :].rearrange("p a c -> p (a c)").bitcast(fmt),
+                scales=scales[:, a0:a1, :].rearrange("p a c -> p (a c)"),
+                in_=values[:, a0:a1, :, :].rearrange("p a c t -> p (a c t)"),
+            )
+
+        def multiply(i, a):
+            nc.tensor.matmul_mx(
+                out=acc[i][:],
+                lhsT=u_codes[i][:, a, :].bitcast(E4M3X4),
+                lhsT_scale=u_scales[i][:, a, :],
+                rhs=g_codes[:, a, :].bitcast(E5M2X4),
+                rhs_scale=g_scales[:, a, :],
+                start=(a == 0),
+                stop=(a == PASSES - 1),
+            )
+
+        def turn_g(i, a):
+            turn_and_weigh(diff[i][a], rb_col[:, a, :], g_bf[:, a, i * P : (i + 1) * P, :])
+
+        step = [keep.tile([P, N], F32, name=f"step{i}") for i in range(2)]
+        size = [keep.tile([P, N], F32, name=f"size{i}") for i in range(2)]
+        root = [keep.tile([P, N], F32, name=f"root{i}") for i in range(2)]
+        half = [keep.tile([P, N], F32, name=f"half{i}") for i in range(2)]
+        soft = [keep.tile([P, N], F32, name=f"soft{i}") for i in range(2)]
+        new = [keep.tile([P, N], F32, name=f"new{i}") for i in range(2)]
+
+        def finish(i, c0, c1):
+            cols = slice(c0, c1)
+            nc.vector.scalar_tensor_tensor(step[i][:, cols], mom_sb[:, i, cols], 0.6 / 0.04, acc[i][:, cols], ALU.mult, ALU.add)
+            nc.scalar.activation(size[i][:, cols], step[i][:, cols], ACT.Abs)
+            nc.scalar.activation(root[i][:, cols], size[i][:, cols], ACT.Abs_reciprocal_sqrt, bias=1.0, scale=0.04)
+            nc.vector.scalar_tensor_tensor(half[i][:, cols], step[i][:, cols], -0.04, root[i][:, cols], ALU.mult, ALU.mult)
+            nc.vector.tensor_tensor(soft[i][:, cols], half[i][:, cols], root[i][:, cols], ALU.mult)
+            nc.vector.scalar_tensor_tensor(new[i][:, cols], old_sb[:, i, cols], 0.5, soft[i][:, cols], ALU.mult, ALU.add)
+            nc.sync.dma_start(out[i * P : (i + 1) * P, cols], new[i][:, cols])
+
+        for a in range(PASSES):
+            for t in range(PACK):
+                nc.tensor.transpose(ra_row[a][:, t, :], ra_col[:, a, t : t + 1].to_broadcast([P, P]), ident[:])
+
+        for a in range(PASSES):
+            for c0 in range(0, J_PASS, 256):
+                gather_g3(0, a, c0, c0 + 256)
+                gather_g2(0, a, c0, c0 + 256)
+        gather_g3(1, 0, 0, 512)
+        turn_g(0, 0)
+        gather_g2(1, 0, 0, 512)
+        gather_g3(1, 1, 0, 512)
+        turn_g(0, 1)
+        gather_g2(1, 1, 0, 512)
+        gather_x(0, 0)
+        turn_g(1, 0)
+        gather_x(0, 1)
+        turn_and_weigh(picked[0][0], ra_col[:, 0, :], u_bf[0][:, 0, :, :])
+        turn_g(1, 1)
+        gather_x(1, 0)
+        turn_and_weigh(picked[0][1], ra_col[:, 1, :], u_bf[0][:, 1, :, :])
+        quantize(g_codes, g_scales, g_bf, E5M2X4, 0, 2)
+        gather_x(1, 1)
+        weigh_and_turn(picked[1][0], ra_row[0], u_bf[1][:, 0, :, :], "rounded0")
+        quantize(u_codes[0], u_scales[0], u_bf[0], E4M3X4, 0, 2)
+        weigh_and_turn(picked[1][1], ra_row[1], u_bf[1][:, 1, :, :], "rounded1")
+        multiply(0, 0)
+        multiply(0, 1)
+        quantize(u_codes[1], u_scales[1], u_bf[1], E4M3X4, 0, 1)
+        quantize(u_codes[1], u_scales[1], u_bf[1], E4M3X4, 1, 2)
+        multiply(1, 0)
+        multiply(1, 1)
+        finish(0, 0, N)
+        finish(1, 0, N // 2)
+        finish(1, N // 2, N)

@@ -48,8 +48,8 @@ def tile_list_moment_headpicks_differences_momentum_kernel(tc, xf, ra, gt, rb, m
         mom_sb = keep.tile([P, 2, N], F32, name="mom_sb")
         old_sb = keep.tile([P, 2, N], F32, name="old_sb")
         nc.sync.dma_start(g_rows[0][:], gt[0:P, :])
-        nc.sync.dma_start(rb_col[:], rb.rearrange("o (g p t) -> p (o g) t", p=P, t=PACK))
-        nc.sync.dma_start(ra_col[:], ra.rearrange("o (g p t) -> p (o g) t", p=P, t=PACK))
+        nc.scalar.dma_start(rb_col[:], rb.rearrange("o (g p t) -> p (o g) t", p=P, t=PACK))
+        nc.scalar.dma_start(ra_col[:], ra.rearrange("o (g p t) -> p (o g) t", p=P, t=PACK))
         nc.sync.dma_start(list_x[:], offs)
         nc.sync.dma_start(g_rows[1][:], gt[P : 2 * P, :])
         nc.sync.dma_start(x_rows[0][:], xf[0:P, :])
@@ -63,13 +63,13 @@ def tile_list_moment_headpicks_differences_momentum_kernel(tc, xf, ra, gt, rb, m
         def entries(lst, j0, j1):
             return lst[:, j0 // LIST_ROWS : j1 // LIST_ROWS]
 
-        minus3 = [[keep.tile([P, J_PASS], F32, name=f"minus3_{i}{a}") for a in range(PASSES)] for i in range(2)]
+        minus3 = [[keep.tile([P, J_PASS], F32, name=f"minus3_{i}{a}", align_bytes=64) for a in range(PASSES)] for i in range(2)]
         diff = [[keep.tile([P, J_PASS], F32, name=f"diff_{i}{a}") for a in range(PASSES)] for i in range(2)]
-        picked = [[keep.tile([P, J_PASS], F32, name=f"picked_{i}{a}") for a in range(PASSES)] for i in range(2)]
-        g_bf = keep.tile([P, PASSES, N, PACK], BF16, name="g_bf", align_bytes=64)
-        g_codes = keep.tile([P, PASSES, N], U32, name="g_codes", align_bytes=64)
+        picked = [[keep.tile([P, J_PASS], F32, name=f"picked_{i}{a}", align_bytes=64)[:] for a in range(PASSES)] for i in range(2)]
+        g_bf = {}
+        g_bf_buffer = {(0, 0): "g_bf00", (1, 0): "g_bf10", (0, 1): "minus3_10", (1, 1): "picked_00"}
         g_scales = keep.tile([P, PASSES, N], U8, name="g_scales", align_bytes=64)
-        u_bf = [keep.tile([P, PASSES, P, PACK], BF16, name=f"u_bf{i}", align_bytes=64) for i in range(2)]
+        u_bf = {1: keep.tile([P, PASSES, P, PACK], BF16, name="u_bf1", align_bytes=64)}
         u_codes = [keep.tile([P, PASSES, P], U32, name=f"u_codes{i}", align_bytes=64) for i in range(2)]
         u_scales = [keep.tile([P, PASSES, P], U8, name=f"u_scales{i}", align_bytes=64) for i in range(2)]
         acc = [held.tile([P, N], F32, name=f"acc{i}") for i in range(2)]
@@ -93,38 +93,27 @@ def tile_list_moment_headpicks_differences_momentum_kernel(tc, xf, ra, gt, rb, m
 
         def gather_x(i, a):
             nc.scalar.activation(
-                picked[i][a][:],
+                picked[i][a],
                 x_rows[i][:].indirect(entries(list_x, a * J_PASS, (a + 1) * J_PASS)),
                 ACT.Copy,
             )
 
-        def turn_and_weigh(src, weight_col, dst):
-            bank = turn.tile([P, PACK, P], F32, name="bank")
-            by_slot = src[:].rearrange("c (p t) -> c t p", t=PACK)
-            for t in range(PACK):
-                nc.tensor.transpose(bank[:, t, :], by_slot[:, t, :], ident[:])
-            nc.vector.tensor_tensor(
-                dst,
-                bank[:].rearrange("p t c -> p c t"),
-                weight_col.unsqueeze(1).to_broadcast([P, P, PACK]),
-                ALU.mult,
-            )
-
-        def weigh_and_turn(src, weight_row, dst, name):
+        def weigh_and_turn(src, weight_row, bank_part, name):
             rounded = keep.tile([P, P, PACK], BF16, name=name)
             nc.vector.tensor_tensor(
                 rounded[:],
-                src[:].rearrange("c (p t) -> c p t", t=PACK),
+                src.rearrange("c (p t) -> c p t", t=PACK),
                 weight_row[:].rearrange("c t p -> c p t"),
                 ALU.mult,
             )
             words = rounded[:].rearrange("c p t -> c (p t)").bitcast(F32).rearrange("c (p u) -> c u p", u=2)
-            bank = turn.tile([P, PACK, P], F32, name="bank")
             for u in range(2):
-                nc.tensor.transpose(bank[:, u, :], words[:, u, :], ident[:])
+                nc.tensor.transpose(bank_part[:, u, :], words[:, u, :], ident[:])
+
+        def weave(i, a0, a1, bank):
             nc.scalar.copy(
-                dst.rearrange("p c t -> p (c t)").bitcast(F32).rearrange("p (c u) -> p c u", u=2),
-                bank[:, 0:2, :].rearrange("p u c -> p c u"),
+                u_bf[i][:, a0:a1, :, :].rearrange("p a c t -> p (a c t)").bitcast(F32).rearrange("p (a c u) -> p a c u", u=2, c=P),
+                bank[:, 0 : 2 * (a1 - a0), :].rearrange("p (a u) c -> p a c u", u=2),
             )
 
         def quantize(codes, scales, values, fmt, a0, a1):
@@ -145,8 +134,22 @@ def tile_list_moment_headpicks_differences_momentum_kernel(tc, xf, ra, gt, rb, m
                 stop=(a == PASSES - 1),
             )
 
+        g_bank = {}
+
         def turn_g(i, a):
-            turn_and_weigh(diff[i][a], rb_col[:, a, :], g_bf[:, a, i * P : (i + 1) * P, :])
+            g_bank[i, a] = turn.tile([P, PACK, P], F32, name="bank")
+            by_slot = diff[i][a][:].rearrange("c (p t) -> c t p", t=PACK)
+            for t in range(PACK):
+                nc.tensor.transpose(g_bank[i, a][:, t, :], by_slot[:, t, :], ident[:])
+
+        def weigh_g(i, a):
+            g_bf[i, a] = keep.tile([P, P, PACK], BF16, name=g_bf_buffer[i, a], align_bytes=64)
+            nc.vector.tensor_tensor(
+                g_bf[i, a][:],
+                g_bank[i, a][:].rearrange("p t c -> p c t"),
+                rb_col[:, a, :].unsqueeze(1).to_broadcast([P, P, PACK]),
+                ALU.mult,
+            )
 
         step = [keep.tile([P, N], F32, name=f"step{i}") for i in range(2)]
         size = [keep.tile([P, N], F32, name=f"size{i}") for i in range(2)]
@@ -155,14 +158,18 @@ def tile_list_moment_headpicks_differences_momentum_kernel(tc, xf, ra, gt, rb, m
         soft = [keep.tile([P, N], F32, name=f"soft{i}") for i in range(2)]
         new = [keep.tile([P, N], F32, name=f"new{i}") for i in range(2)]
 
-        def finish(i, c0, c1):
+        def finish(i, c0, c1, square_on_scalar):
             cols = slice(c0, c1)
             nc.vector.scalar_tensor_tensor(step[i][:, cols], mom_sb[:, i, cols], 0.6 / 0.04, acc[i][:, cols], ALU.mult, ALU.add)
             nc.scalar.activation(size[i][:, cols], step[i][:, cols], ACT.Abs)
-            nc.scalar.activation(root[i][:, cols], size[i][:, cols], ACT.Abs_reciprocal_sqrt, bias=1.0, scale=0.04)
-            nc.vector.scalar_tensor_tensor(half[i][:, cols], step[i][:, cols], -0.04, root[i][:, cols], ALU.mult, ALU.mult)
-            nc.vector.tensor_tensor(soft[i][:, cols], half[i][:, cols], root[i][:, cols], ALU.mult)
-            nc.vector.scalar_tensor_tensor(new[i][:, cols], old_sb[:, i, cols], 0.5, soft[i][:, cols], ALU.mult, ALU.add)
+            nc.scalar.activation(root[i][:, cols], size[i][:, cols], ACT.Abs_reciprocal_sqrt, bias=1 / 0.04)
+            if square_on_scalar:
+                nc.scalar.activation(half[i][:, cols], root[i][:, cols], ACT.Square)
+                nc.vector.tensor_tensor(soft[i][:, cols], half[i][:, cols], step[i][:, cols], ALU.mult)
+            else:
+                nc.vector.tensor_tensor(half[i][:, cols], step[i][:, cols], root[i][:, cols], ALU.mult)
+                nc.vector.tensor_tensor(soft[i][:, cols], half[i][:, cols], root[i][:, cols], ALU.mult)
+            nc.vector.scalar_tensor_tensor(new[i][:, cols], old_sb[:, i, cols], 0.5, soft[i][:, cols], ALU.mult, ALU.subtract)
             nc.sync.dma_start(out[i * P : (i + 1) * P, cols], new[i][:, cols])
 
         for a in range(PASSES):
@@ -175,28 +182,44 @@ def tile_list_moment_headpicks_differences_momentum_kernel(tc, xf, ra, gt, rb, m
                 gather_g2(0, a, c0, c0 + 256)
         gather_g3(1, 0, 0, 512)
         turn_g(0, 0)
+        turn_g(0, 1)
+        weigh_g(0, 0)
         gather_g2(1, 0, 0, 512)
         gather_g3(1, 1, 0, 512)
-        turn_g(0, 1)
-        gather_g2(1, 1, 0, 512)
-        gather_x(0, 0)
+        for i in range(2):
+            for a in range(PASSES):
+                gather_x(i, a)
         turn_g(1, 0)
-        gather_x(0, 1)
-        turn_and_weigh(picked[0][0], ra_col[:, 0, :], u_bf[0][:, 0, :, :])
+        weigh_g(0, 1)
+        gather_g2(1, 1, 0, 512)
         turn_g(1, 1)
-        gather_x(1, 0)
-        turn_and_weigh(picked[0][1], ra_col[:, 1, :], u_bf[0][:, 1, :, :])
-        quantize(g_codes, g_scales, g_bf, E5M2X4, 0, 2)
-        gather_x(1, 1)
-        weigh_and_turn(picked[1][0], ra_row[0], u_bf[1][:, 0, :, :], "rounded0")
+        weigh_g(1, 0)
+        bank0 = turn.tile([P, PACK, P], F32, name="bank")
+        weigh_and_turn(picked[0][0], ra_row[0], bank0[:, 0:2, :], "rounded00")
+        weigh_g(1, 1)
+        weigh_and_turn(picked[0][1], ra_row[1], bank0[:, 2:4, :], "rounded01")
+        bank1 = [turn.tile([P, PACK, P], F32, name="bank") for a in range(PASSES)]
+        for a in range(PASSES):
+            weigh_and_turn(picked[1][a], ra_row[a], bank1[a][:, 0:2, :], f"rounded1{a}")
+        u_bf[0] = keep.tile([P, PASSES, P, PACK], BF16, name="picked_10", align_bytes=64)
+        weave(0, 0, 2, bank0)
+        for a in range(PASSES):
+            weave(1, a, a + 1, bank1[a])
+        g_codes = keep.tile([P, PASSES, N], U32, name="picked_11", align_bytes=64)
+        for a in range(PASSES):
+            for i in range(2):
+                cols = slice(i * P, (i + 1) * P)
+                nc.vector.quantize_mx(
+                    out=g_codes[:, a, cols].bitcast(E5M2X4),
+                    scales=g_scales[:, a, cols],
+                    in_=g_bf[i, a][:].rearrange("p c t -> p (c t)"),
+                )
         quantize(u_codes[0], u_scales[0], u_bf[0], E4M3X4, 0, 2)
-        weigh_and_turn(picked[1][1], ra_row[1], u_bf[1][:, 1, :, :], "rounded1")
         multiply(0, 0)
         multiply(0, 1)
         quantize(u_codes[1], u_scales[1], u_bf[1], E4M3X4, 0, 1)
         quantize(u_codes[1], u_scales[1], u_bf[1], E4M3X4, 1, 2)
         multiply(1, 0)
         multiply(1, 1)
-        finish(0, 0, N)
-        finish(1, 0, N // 2)
-        finish(1, N // 2, N)
+        finish(0, 0, 256, True)
+        finish(1, 0, 256, True)

@@ -17,10 +17,20 @@ ALU = mybir.AluOpType
 ACT = mybir.ActivationFunctionType
 
 P = 128
+TILES = 2
 PACK = 4
 J_PASS = P * PACK
 PASSES = J // J_PASS
 LIST_ROWS = 16
+MX_ALIGN = 64
+TURN_BANKS = 4
+FIRST_SLICES = (128, 256)
+HALF = N // 2
+
+SECOND = 0.7
+RATE = 0.04
+MOMENTUM = 0.6
+KEEP = 0.5
 
 
 def tile_list_moment_headpicks_differences_momentum_kernel(tc, xf, ra, gt, rb, mom, old, offs, offs2, offs3, out):
@@ -28,28 +38,28 @@ def tile_list_moment_headpicks_differences_momentum_kernel(tc, xf, ra, gt, rb, m
     with ExitStack() as ctx:
         lists = ctx.enter_context(tc.tile_pool(name="lists", bufs=1))
         keep = ctx.enter_context(tc.tile_pool(name="keep", bufs=1))
-        turn = ctx.enter_context(tc.psum_pool(name="turn", bufs=4))
+        turn = ctx.enter_context(tc.psum_pool(name="turn", bufs=TURN_BANKS))
         held = ctx.enter_context(tc.psum_pool(name="held", bufs=1))
 
         list_x = lists.tile([P, J // LIST_ROWS], U16, name="list_x")
         list_g2 = lists.tile([P, J // LIST_ROWS], U16, name="list_g2")
         list_g3 = lists.tile([P, J // LIST_ROWS], U16, name="list_g3")
-        nc.sync.dma_start(list_g3[:], offs3)
-        nc.sync.dma_start(list_g2[:], offs2)
 
         warm = keep.tile([P, 2], F32, name="warm")
         nc.vector.memset(warm[:, 0:1], 1.0)
-        nc.scalar.activation(warm[:, 1:2], warm[:, 0:1], ACT.Abs_reciprocal_sqrt, bias=1.0, scale=0.04)
+        nc.scalar.activation(warm[:, 1:2], warm[:, 0:1], ACT.Abs_reciprocal_sqrt, bias=1.0, scale=RATE)
 
-        g_rows = [keep.tile([P, T], F32, name=f"g_rows{i}") for i in range(2)]
-        x_rows = [keep.tile([P, T], F32, name=f"x_rows{i}") for i in range(2)]
+        g_rows = [keep.tile([P, T], F32, name=f"g_rows{i}") for i in range(TILES)]
+        x_rows = [keep.tile([P, T], F32, name=f"x_rows{i}") for i in range(TILES)]
         ra_col = keep.tile([P, PASSES, PACK], F32, name="ra_col")
         rb_col = keep.tile([P, PASSES, PACK], F32, name="rb_col")
-        mom_sb = keep.tile([P, 2, N], F32, name="mom_sb")
-        old_sb = keep.tile([P, 2, N], F32, name="old_sb")
+        mom_sb = keep.tile([P, TILES, N], F32, name="mom_sb")
+        old_sb = keep.tile([P, TILES, N], F32, name="old_sb")
         nc.sync.dma_start(g_rows[0][:], gt[0:P, :])
-        nc.scalar.dma_start(rb_col[:], rb.rearrange("o (g p t) -> p (o g) t", p=P, t=PACK))
-        nc.scalar.dma_start(ra_col[:], ra.rearrange("o (g p t) -> p (o g) t", p=P, t=PACK))
+        nc.sync.dma_start(list_g3[:], offs3)
+        nc.sync.dma_start(list_g2[:], offs2)
+        nc.scalar.dma_start(rb_col[:], rb.rearrange("o (a p t) -> p (o a) t", p=P, t=PACK))
+        nc.scalar.dma_start(ra_col[:], ra.rearrange("o (a p t) -> p (o a) t", p=P, t=PACK))
         nc.sync.dma_start(list_x[:], offs)
         nc.sync.dma_start(g_rows[1][:], gt[P : 2 * P, :])
         nc.sync.dma_start(x_rows[0][:], xf[0:P, :])
@@ -60,19 +70,23 @@ def tile_list_moment_headpicks_differences_momentum_kernel(tc, xf, ra, gt, rb, m
         ident = keep.tile([P, P], F32, name="ident")
         make_identity(nc, ident[:])
 
-        def entries(lst, j0, j1):
-            return lst[:, j0 // LIST_ROWS : j1 // LIST_ROWS]
+        def entries(list_tile, j0, j1):
+            return list_tile[:, j0 // LIST_ROWS : j1 // LIST_ROWS]
 
-        minus3 = [[keep.tile([P, J_PASS], F32, name=f"minus3_{i}{a}", align_bytes=64) for a in range(PASSES)] for i in range(2)]
-        diff = [[keep.tile([P, J_PASS], F32, name=f"diff_{i}{a}") for a in range(PASSES)] for i in range(2)]
-        picked = [[keep.tile([P, J_PASS], F32, name=f"picked_{i}{a}", align_bytes=64)[:] for a in range(PASSES)] for i in range(2)]
+        def staged(name, **align):
+            return [[keep.tile([P, J_PASS], F32, name=f"{name}_{i}{a}", **align) for a in range(PASSES)] for i in range(TILES)]
+
+        minus3 = staged("minus3", align_bytes=MX_ALIGN)
+        diff = staged("diff")
+        picked = staged("picked", align_bytes=MX_ALIGN)
+
         g_bf = {}
         g_bf_buffer = {(0, 0): "g_bf00", (1, 0): "g_bf10", (0, 1): "minus3_10", (1, 1): "picked_00"}
-        g_scales = keep.tile([P, PASSES, N], U8, name="g_scales", align_bytes=64)
-        u_bf = {1: keep.tile([P, PASSES, P, PACK], BF16, name="u_bf1", align_bytes=64)}
-        u_codes = [keep.tile([P, PASSES, P], U32, name=f"u_codes{i}", align_bytes=64) for i in range(2)]
-        u_scales = [keep.tile([P, PASSES, P], U8, name=f"u_scales{i}", align_bytes=64) for i in range(2)]
-        acc = [held.tile([P, N], F32, name=f"acc{i}") for i in range(2)]
+        g_scales = keep.tile([P, PASSES, N], U8, name="g_scales", align_bytes=MX_ALIGN)
+        u_bf = {1: keep.tile([P, PASSES, P, PACK], BF16, name="u_bf1", align_bytes=MX_ALIGN)}
+        u_codes = [keep.tile([P, PASSES, P], U32, name=f"u_codes{i}", align_bytes=MX_ALIGN) for i in range(TILES)]
+        u_scales = [keep.tile([P, PASSES, P], U8, name=f"u_scales{i}", align_bytes=MX_ALIGN) for i in range(TILES)]
+        acc = [held.tile([P, N], F32, name=f"acc{i}") for i in range(TILES)]
         ra_row = [held.tile([P, PACK, P], F32, name=f"ra_row{a}") for a in range(PASSES)]
 
         def gather_g3(i, a, c0, c1):
@@ -80,7 +94,7 @@ def tile_list_moment_headpicks_differences_momentum_kernel(tc, xf, ra, gt, rb, m
                 minus3[i][a][:, c0:c1],
                 g_rows[i][:].indirect(entries(list_g3, a * J_PASS + c0, a * J_PASS + c1)),
                 ACT.Copy,
-                scale=-0.7,
+                scale=-SECOND,
             )
 
         def gather_g2(i, a, c0, c1):
@@ -93,34 +107,51 @@ def tile_list_moment_headpicks_differences_momentum_kernel(tc, xf, ra, gt, rb, m
 
         def gather_x(i, a):
             nc.scalar.activation(
-                picked[i][a],
+                picked[i][a][:],
                 x_rows[i][:].indirect(entries(list_x, a * J_PASS, (a + 1) * J_PASS)),
                 ACT.Copy,
             )
 
-        def weigh_and_turn(src, weight_row, bank_part, name):
-            rounded = keep.tile([P, P, PACK], BF16, name=name)
+        g_bank = {}
+
+        def turn_g(i, a):
+            g_bank[i, a] = turn.tile([P, PACK, P], F32, name="bank")
+            by_slot = diff[i][a][:].rearrange("c (p t) -> c t p", t=PACK)
+            for t in range(PACK):
+                nc.tensor.transpose(g_bank[i, a][:, t, :], by_slot[:, t, :], ident[:])
+
+        def weigh_g(i, a):
+            g_bf[i, a] = keep.tile([P, P, PACK], BF16, name=g_bf_buffer[i, a], align_bytes=MX_ALIGN)
+            nc.vector.tensor_tensor(
+                g_bf[i, a][:],
+                g_bank[i, a][:].rearrange("p t c -> p c t"),
+                rb_col[:, a, :].unsqueeze(1).to_broadcast([P, P, PACK]),
+                ALU.mult,
+            )
+
+        def weigh_and_turn_x(i, a, bank_part):
+            rounded = keep.tile([P, P, PACK], BF16, name=f"rounded{i}{a}")
             nc.vector.tensor_tensor(
                 rounded[:],
-                src.rearrange("c (p t) -> c p t", t=PACK),
-                weight_row[:].rearrange("c t p -> c p t"),
+                picked[i][a][:].rearrange("c (p t) -> c p t", t=PACK),
+                ra_row[a][:].rearrange("c t p -> c p t"),
                 ALU.mult,
             )
             words = rounded[:].rearrange("c p t -> c (p t)").bitcast(F32).rearrange("c (p u) -> c u p", u=2)
             for u in range(2):
                 nc.tensor.transpose(bank_part[:, u, :], words[:, u, :], ident[:])
 
-        def weave(i, a0, a1, bank):
+        def pair_up_x(i, a0, a1, bank):
             nc.scalar.copy(
                 u_bf[i][:, a0:a1, :, :].rearrange("p a c t -> p (a c t)").bitcast(F32).rearrange("p (a c u) -> p a c u", u=2, c=P),
                 bank[:, 0 : 2 * (a1 - a0), :].rearrange("p (a u) c -> p a c u", u=2),
             )
 
-        def quantize(codes, scales, values, fmt, a0, a1):
+        def quantize_x(i, a0, a1):
             nc.vector.quantize_mx(
-                out=codes[:, a0:a1, :].rearrange("p a c -> p (a c)").bitcast(fmt),
-                scales=scales[:, a0:a1, :].rearrange("p a c -> p (a c)"),
-                in_=values[:, a0:a1, :, :].rearrange("p a c t -> p (a c t)"),
+                out=u_codes[i][:, a0:a1, :].rearrange("p a c -> p (a c)").bitcast(E4M3X4),
+                scales=u_scales[i][:, a0:a1, :].rearrange("p a c -> p (a c)"),
+                in_=u_bf[i][:, a0:a1, :, :].rearrange("p a c t -> p (a c t)"),
             )
 
         def multiply(i, a):
@@ -134,42 +165,24 @@ def tile_list_moment_headpicks_differences_momentum_kernel(tc, xf, ra, gt, rb, m
                 stop=(a == PASSES - 1),
             )
 
-        g_bank = {}
+        step = [keep.tile([P, N], F32, name=f"step{i}") for i in range(TILES)]
+        size = [keep.tile([P, N], F32, name=f"size{i}") for i in range(TILES)]
+        root = [keep.tile([P, N], F32, name=f"root{i}") for i in range(TILES)]
+        factor = [keep.tile([P, N], F32, name=f"factor{i}") for i in range(TILES)]
+        soft = [keep.tile([P, N], F32, name=f"soft{i}") for i in range(TILES)]
+        new = [keep.tile([P, N], F32, name=f"new{i}") for i in range(TILES)]
 
-        def turn_g(i, a):
-            g_bank[i, a] = turn.tile([P, PACK, P], F32, name="bank")
-            by_slot = diff[i][a][:].rearrange("c (p t) -> c t p", t=PACK)
-            for t in range(PACK):
-                nc.tensor.transpose(g_bank[i, a][:, t, :], by_slot[:, t, :], ident[:])
-
-        def weigh_g(i, a):
-            g_bf[i, a] = keep.tile([P, P, PACK], BF16, name=g_bf_buffer[i, a], align_bytes=64)
-            nc.vector.tensor_tensor(
-                g_bf[i, a][:],
-                g_bank[i, a][:].rearrange("p t c -> p c t"),
-                rb_col[:, a, :].unsqueeze(1).to_broadcast([P, P, PACK]),
-                ALU.mult,
-            )
-
-        step = [keep.tile([P, N], F32, name=f"step{i}") for i in range(2)]
-        size = [keep.tile([P, N], F32, name=f"size{i}") for i in range(2)]
-        root = [keep.tile([P, N], F32, name=f"root{i}") for i in range(2)]
-        half = [keep.tile([P, N], F32, name=f"half{i}") for i in range(2)]
-        soft = [keep.tile([P, N], F32, name=f"soft{i}") for i in range(2)]
-        new = [keep.tile([P, N], F32, name=f"new{i}") for i in range(2)]
-
-        def finish(i, c0, c1, square_on_scalar):
-            cols = slice(c0, c1)
-            nc.vector.scalar_tensor_tensor(step[i][:, cols], mom_sb[:, i, cols], 0.6 / 0.04, acc[i][:, cols], ALU.mult, ALU.add)
+        def finish(i, cols):
+            nc.vector.scalar_tensor_tensor(step[i][:, cols], mom_sb[:, i, cols], MOMENTUM / RATE, acc[i][:, cols], ALU.mult, ALU.add)
             nc.scalar.activation(size[i][:, cols], step[i][:, cols], ACT.Abs)
-            nc.scalar.activation(root[i][:, cols], size[i][:, cols], ACT.Abs_reciprocal_sqrt, bias=1 / 0.04)
-            if square_on_scalar:
-                nc.scalar.activation(half[i][:, cols], root[i][:, cols], ACT.Square)
-                nc.vector.tensor_tensor(soft[i][:, cols], half[i][:, cols], step[i][:, cols], ALU.mult)
+            nc.scalar.activation(root[i][:, cols], size[i][:, cols], ACT.Abs_reciprocal_sqrt, bias=1 / RATE)
+            if i == 0:
+                nc.vector.tensor_tensor(factor[i][:, cols], step[i][:, cols], root[i][:, cols], ALU.mult)
+                nc.vector.tensor_tensor(soft[i][:, cols], factor[i][:, cols], root[i][:, cols], ALU.mult)
             else:
-                nc.vector.tensor_tensor(half[i][:, cols], step[i][:, cols], root[i][:, cols], ALU.mult)
-                nc.vector.tensor_tensor(soft[i][:, cols], half[i][:, cols], root[i][:, cols], ALU.mult)
-            nc.vector.scalar_tensor_tensor(new[i][:, cols], old_sb[:, i, cols], 0.5, soft[i][:, cols], ALU.mult, ALU.subtract)
+                nc.scalar.activation(factor[i][:, cols], root[i][:, cols], ACT.Square)
+                nc.vector.tensor_tensor(soft[i][:, cols], factor[i][:, cols], step[i][:, cols], ALU.mult)
+            nc.vector.scalar_tensor_tensor(new[i][:, cols], old_sb[:, i, cols], KEEP, soft[i][:, cols], ALU.mult, ALU.subtract)
             nc.sync.dma_start(out[i * P : (i + 1) * P, cols], new[i][:, cols])
 
         for a in range(PASSES):
@@ -177,49 +190,53 @@ def tile_list_moment_headpicks_differences_momentum_kernel(tc, xf, ra, gt, rb, m
                 nc.tensor.transpose(ra_row[a][:, t, :], ra_col[:, a, t : t + 1].to_broadcast([P, P]), ident[:])
 
         for a in range(PASSES):
-            for c0 in range(0, J_PASS, 256):
-                gather_g3(0, a, c0, c0 + 256)
-                gather_g2(0, a, c0, c0 + 256)
-        gather_g3(1, 0, 0, 512)
+            for c0 in range(0, J_PASS, FIRST_SLICES[a]):
+                gather_g3(0, a, c0, c0 + FIRST_SLICES[a])
+                gather_g2(0, a, c0, c0 + FIRST_SLICES[a])
+        gather_g3(1, 0, 0, J_PASS)
         turn_g(0, 0)
         turn_g(0, 1)
         weigh_g(0, 0)
-        gather_g2(1, 0, 0, 512)
-        gather_g3(1, 1, 0, 512)
-        for i in range(2):
+        gather_g2(1, 0, 0, J_PASS)
+        gather_g3(1, 1, 0, J_PASS)
+        for i in range(TILES):
             for a in range(PASSES):
                 gather_x(i, a)
         turn_g(1, 0)
         weigh_g(0, 1)
-        gather_g2(1, 1, 0, 512)
+        gather_g2(1, 1, 0, J_PASS)
         turn_g(1, 1)
         weigh_g(1, 0)
-        bank0 = turn.tile([P, PACK, P], F32, name="bank")
-        weigh_and_turn(picked[0][0], ra_row[0], bank0[:, 0:2, :], "rounded00")
+
+        x_bank0 = turn.tile([P, PACK, P], F32, name="bank")
+        weigh_and_turn_x(0, 0, x_bank0[:, 0:2, :])
         weigh_g(1, 1)
-        weigh_and_turn(picked[0][1], ra_row[1], bank0[:, 2:4, :], "rounded01")
-        bank1 = [turn.tile([P, PACK, P], F32, name="bank") for a in range(PASSES)]
+        weigh_and_turn_x(0, 1, x_bank0[:, 2:4, :])
+        x_bank1 = [turn.tile([P, PACK, P], F32, name="bank") for a in range(PASSES)]
         for a in range(PASSES):
-            weigh_and_turn(picked[1][a], ra_row[a], bank1[a][:, 0:2, :], f"rounded1{a}")
-        u_bf[0] = keep.tile([P, PASSES, P, PACK], BF16, name="picked_10", align_bytes=64)
-        weave(0, 0, 2, bank0)
+            weigh_and_turn_x(1, a, x_bank1[a][:, 0:2, :])
+        u_bf[0] = keep.tile([P, PASSES, P, PACK], BF16, name="u_bf0", align_bytes=MX_ALIGN)
+        pair_up_x(0, 0, PASSES, x_bank0)
         for a in range(PASSES):
-            weave(1, a, a + 1, bank1[a])
-        g_codes = keep.tile([P, PASSES, N], U32, name="picked_11", align_bytes=64)
+            pair_up_x(1, a, a + 1, x_bank1[a])
+
+        g_codes = keep.tile([P, PASSES, N], U32, name="picked_11", align_bytes=MX_ALIGN)
         for a in range(PASSES):
-            for i in range(2):
+            for i in range(TILES):
                 cols = slice(i * P, (i + 1) * P)
                 nc.vector.quantize_mx(
                     out=g_codes[:, a, cols].bitcast(E5M2X4),
                     scales=g_scales[:, a, cols],
                     in_=g_bf[i, a][:].rearrange("p c t -> p (c t)"),
                 )
-        quantize(u_codes[0], u_scales[0], u_bf[0], E4M3X4, 0, 2)
-        multiply(0, 0)
-        multiply(0, 1)
-        quantize(u_codes[1], u_scales[1], u_bf[1], E4M3X4, 0, 1)
-        quantize(u_codes[1], u_scales[1], u_bf[1], E4M3X4, 1, 2)
-        multiply(1, 0)
-        multiply(1, 1)
-        finish(0, 0, 256, True)
-        finish(1, 0, 256, True)
+        quantize_x(0, 0, PASSES)
+        for a in range(PASSES):
+            multiply(0, a)
+        for a in range(PASSES):
+            quantize_x(1, a, a + 1)
+        for a in range(PASSES):
+            multiply(1, a)
+
+        for i in range(TILES):
+            for c0 in range(0, N, HALF):
+                finish(i, slice(c0, c0 + HALF))

from contextlib import ExitStack

import concourse.mybir as mybir
from concourse.masks import make_identity

K, J, N, T = 256, 1024, 256, 2048
FLOPS = 2 * K * J * N

F32 = mybir.dt.float32
BF16 = mybir.dt.bfloat16
U32 = mybir.dt.uint32
U16 = mybir.dt.uint16
U8 = mybir.dt.uint8
E4M3X4 = mybir.dt.float8_e4m3fn_x4
E5M2X4 = mybir.dt.float8_e5m2_x4
ALU = mybir.AluOpType
ACT = mybir.ActivationFunctionType

P = 128
TILES = 2
PACK = 4
J_PASS = P * PACK
PASSES = J // J_PASS
LIST_ROWS = 16
MX_ALIGN = 64
TURN_BANKS = 4
FIRST_SLICES = (128, 256)
HALF = N // 2

SECOND = 0.7
RATE = 0.04
MOMENTUM = 0.6
KEEP = 0.5


def tile_list_moment_headpicks_differences_momentum_kernel(tc, xf, ra, gt, rb, mom, old, offs, offs2, offs3, out):
    nc = tc.nc
    with ExitStack() as ctx:
        lists = ctx.enter_context(tc.tile_pool(name="lists", bufs=1))
        keep = ctx.enter_context(tc.tile_pool(name="keep", bufs=1))
        turn = ctx.enter_context(tc.psum_pool(name="turn", bufs=TURN_BANKS))
        held = ctx.enter_context(tc.psum_pool(name="held", bufs=1))

        list_x = lists.tile([P, J // LIST_ROWS], U16, name="list_x")
        list_g2 = lists.tile([P, J // LIST_ROWS], U16, name="list_g2")
        list_g3 = lists.tile([P, J // LIST_ROWS], U16, name="list_g3")

        warm = keep.tile([P, 2], F32, name="warm")
        nc.vector.memset(warm[:, 0:1], 1.0)
        nc.scalar.activation(warm[:, 1:2], warm[:, 0:1], ACT.Abs_reciprocal_sqrt, bias=1.0, scale=RATE)

        g_rows = [keep.tile([P, T], F32, name=f"g_rows{i}") for i in range(TILES)]
        x_rows = [keep.tile([P, T], F32, name=f"x_rows{i}") for i in range(TILES)]
        ra_col = keep.tile([P, PASSES, PACK], F32, name="ra_col")
        rb_col = keep.tile([P, PASSES, PACK], F32, name="rb_col")
        mom_sb = keep.tile([P, TILES, N], F32, name="mom_sb")
        old_sb = keep.tile([P, TILES, N], F32, name="old_sb")
        nc.sync.dma_start(g_rows[0][:], gt[0:P, :])
        nc.sync.dma_start(list_g3[:], offs3)
        nc.sync.dma_start(list_g2[:], offs2)
        nc.scalar.dma_start(rb_col[:], rb.rearrange("o (a p t) -> p (o a) t", p=P, t=PACK))
        nc.scalar.dma_start(ra_col[:], ra.rearrange("o (a p t) -> p (o a) t", p=P, t=PACK))
        nc.sync.dma_start(list_x[:], offs)
        nc.sync.dma_start(g_rows[1][:], gt[P : 2 * P, :])
        nc.sync.dma_start(x_rows[0][:], xf[0:P, :])
        nc.sync.dma_start(x_rows[1][:], xf[P : 2 * P, :])
        nc.sync.dma_start(mom_sb[:], mom.rearrange("(i p) n -> p i n", p=P))
        nc.sync.dma_start(old_sb[:], old.rearrange("(i p) n -> p i n", p=P))

        ident = keep.tile([P, P], F32, name="ident")
        make_identity(nc, ident[:])

        def entries(list_tile, j0, j1):
            return list_tile[:, j0 // LIST_ROWS : j1 // LIST_ROWS]

        def staged(name, **align):
            return [[keep.tile([P, J_PASS], F32, name=f"{name}_{i}{a}", **align) for a in range(PASSES)] for i in range(TILES)]

        minus3 = staged("minus3", align_bytes=MX_ALIGN)
        diff = staged("diff")
        picked = staged("picked", align_bytes=MX_ALIGN)

        g_bf = {}
        g_bf_buffer = {(0, 0): "g_bf00", (1, 0): "g_bf10", (0, 1): "minus3_10", (1, 1): "picked_00"}
        g_scales = keep.tile([P, PASSES, N], U8, name="g_scales", align_bytes=MX_ALIGN)
        u_bf = {1: keep.tile([P, PASSES, P, PACK], BF16, name="u_bf1", align_bytes=MX_ALIGN)}
        u_codes = [keep.tile([P, PASSES, P], U32, name=f"u_codes{i}", align_bytes=MX_ALIGN) for i in range(TILES)]
        u_scales = [keep.tile([P, PASSES, P], U8, name=f"u_scales{i}", align_bytes=MX_ALIGN) for i in range(TILES)]
        acc = [held.tile([P, N], F32, name=f"acc{i}") for i in range(TILES)]
        ra_row = [held.tile([P, PACK, P], F32, name=f"ra_row{a}") for a in range(PASSES)]

        def gather_g3(i, a, c0, c1):
            nc.scalar.activation(
                minus3[i][a][:, c0:c1],
                g_rows[i][:].indirect(entries(list_g3, a * J_PASS + c0, a * J_PASS + c1)),
                ACT.Copy,
                scale=-SECOND,
            )

        def gather_g2(i, a, c0, c1):
            nc.vector.tensor_tensor(
                diff[i][a][:, c0:c1],
                g_rows[i][:].indirect(entries(list_g2, a * J_PASS + c0, a * J_PASS + c1)),
                minus3[i][a][:, c0:c1],
                ALU.add,
            )

        def gather_x(i, a):
            nc.scalar.activation(
                picked[i][a][:],
                x_rows[i][:].indirect(entries(list_x, a * J_PASS, (a + 1) * J_PASS)),
                ACT.Copy,
            )

        g_bank = {}

        def turn_g(i, a):
            g_bank[i, a] = turn.tile([P, PACK, P], F32, name="bank")
            by_slot = diff[i][a][:].rearrange("c (p t) -> c t p", t=PACK)
            for t in range(PACK):
                nc.tensor.transpose(g_bank[i, a][:, t, :], by_slot[:, t, :], ident[:])

        def weigh_g(i, a):
            g_bf[i, a] = keep.tile([P, P, PACK], BF16, name=g_bf_buffer[i, a], align_bytes=MX_ALIGN)
            nc.vector.tensor_tensor(
                g_bf[i, a][:],
                g_bank[i, a][:].rearrange("p t c -> p c t"),
                rb_col[:, a, :].unsqueeze(1).to_broadcast([P, P, PACK]),
                ALU.mult,
            )

        def weigh_and_turn_x(i, a, bank_part):
            rounded = keep.tile([P, P, PACK], BF16, name=f"rounded{i}{a}")
            nc.vector.tensor_tensor(
                rounded[:],
                picked[i][a][:].rearrange("c (p t) -> c p t", t=PACK),
                ra_row[a][:].rearrange("c t p -> c p t"),
                ALU.mult,
            )
            words = rounded[:].rearrange("c p t -> c (p t)").bitcast(F32).rearrange("c (p u) -> c u p", u=2)
            for u in range(2):
                nc.tensor.transpose(bank_part[:, u, :], words[:, u, :], ident[:])

        def pair_up_x(i, a0, a1, bank):
            nc.scalar.copy(
                u_bf[i][:, a0:a1, :, :].rearrange("p a c t -> p (a c t)").bitcast(F32).rearrange("p (a c u) -> p a c u", u=2, c=P),
                bank[:, 0 : 2 * (a1 - a0), :].rearrange("p (a u) c -> p a c u", u=2),
            )

        def quantize_x(i, a0, a1):
            nc.vector.quantize_mx(
                out=u_codes[i][:, a0:a1, :].rearrange("p a c -> p (a c)").bitcast(E4M3X4),
                scales=u_scales[i][:, a0:a1, :].rearrange("p a c -> p (a c)"),
                in_=u_bf[i][:, a0:a1, :, :].rearrange("p a c t -> p (a c t)"),
            )

        def multiply(i, a):
            nc.tensor.matmul_mx(
                out=acc[i][:],
                lhsT=u_codes[i][:, a, :].bitcast(E4M3X4),
                lhsT_scale=u_scales[i][:, a, :],
                rhs=g_codes[:, a, :].bitcast(E5M2X4),
                rhs_scale=g_scales[:, a, :],
                start=(a == 0),
                stop=(a == PASSES - 1),
            )

        step = [keep.tile([P, N], F32, name=f"step{i}") for i in range(TILES)]
        size = [keep.tile([P, N], F32, name=f"size{i}") for i in range(TILES)]
        root = [keep.tile([P, N], F32, name=f"root{i}") for i in range(TILES)]
        factor = [keep.tile([P, N], F32, name=f"factor{i}") for i in range(TILES)]
        soft = [keep.tile([P, N], F32, name=f"soft{i}") for i in range(TILES)]
        new = [keep.tile([P, N], F32, name=f"new{i}") for i in range(TILES)]

        def finish(i, cols):
            nc.vector.scalar_tensor_tensor(step[i][:, cols], mom_sb[:, i, cols], MOMENTUM / RATE, acc[i][:, cols], ALU.mult, ALU.add)
            nc.scalar.activation(size[i][:, cols], step[i][:, cols], ACT.Abs)
            nc.scalar.activation(root[i][:, cols], size[i][:, cols], ACT.Abs_reciprocal_sqrt, bias=1 / RATE)
            if i == 0:
                nc.vector.tensor_tensor(factor[i][:, cols], step[i][:, cols], root[i][:, cols], ALU.mult)
                nc.vector.tensor_tensor(soft[i][:, cols], factor[i][:, cols], root[i][:, cols], ALU.mult)
            else:
                nc.scalar.activation(factor[i][:, cols], root[i][:, cols], ACT.Square)
                nc.vector.tensor_tensor(soft[i][:, cols], factor[i][:, cols], step[i][:, cols], ALU.mult)
            nc.vector.scalar_tensor_tensor(new[i][:, cols], old_sb[:, i, cols], KEEP, soft[i][:, cols], ALU.mult, ALU.subtract)
            nc.sync.dma_start(out[i * P : (i + 1) * P, cols], new[i][:, cols])

        for a in range(PASSES):
            for t in range(PACK):
                nc.tensor.transpose(ra_row[a][:, t, :], ra_col[:, a, t : t + 1].to_broadcast([P, P]), ident[:])

        for a in range(PASSES):
            for c0 in range(0, J_PASS, FIRST_SLICES[a]):
                gather_g3(0, a, c0, c0 + FIRST_SLICES[a])
                gather_g2(0, a, c0, c0 + FIRST_SLICES[a])
        gather_g3(1, 0, 0, J_PASS)
        turn_g(0, 0)
        turn_g(0, 1)
        weigh_g(0, 0)
        gather_g2(1, 0, 0, J_PASS)
        gather_g3(1, 1, 0, J_PASS)
        for i in range(TILES):
            for a in range(PASSES):
                gather_x(i, a)
        turn_g(1, 0)
        weigh_g(0, 1)
        gather_g2(1, 1, 0, J_PASS)
        turn_g(1, 1)
        weigh_g(1, 0)

        x_bank0 = turn.tile([P, PACK, P], F32, name="bank")
        weigh_and_turn_x(0, 0, x_bank0[:, 0:2, :])
        weigh_g(1, 1)
        weigh_and_turn_x(0, 1, x_bank0[:, 2:4, :])
        x_bank1 = [turn.tile([P, PACK, P], F32, name="bank") for a in range(PASSES)]
        for a in range(PASSES):
            weigh_and_turn_x(1, a, x_bank1[a][:, 0:2, :])
        u_bf[0] = keep.tile([P, PASSES, P, PACK], BF16, name="u_bf0", align_bytes=MX_ALIGN)
        pair_up_x(0, 0, PASSES, x_bank0)
        for a in range(PASSES):
            pair_up_x(1, a, a + 1, x_bank1[a])

        g_codes = keep.tile([P, PASSES, N], U32, name="picked_11", align_bytes=MX_ALIGN)
        for a in range(PASSES):
            for i in range(TILES):
                cols = slice(i * P, (i + 1) * P)
                nc.vector.quantize_mx(
                    out=g_codes[:, a, cols].bitcast(E5M2X4),
                    scales=g_scales[:, a, cols],
                    in_=g_bf[i, a][:].rearrange("p c t -> p (c t)"),
                )
        quantize_x(0, 0, PASSES)
        for a in range(PASSES):
            multiply(0, a)
        for a in range(PASSES):
            quantize_x(1, a, a + 1)
        for a in range(PASSES):
            multiply(1, a)

        for i in range(TILES):
            for c0 in range(0, N, HALF):
                finish(i, slice(c0, c0 + HALF))
